import numpy as np
CORES = [0,1,2,3,4,5,6,7]
N = 8
T, K = 512, 3
ROUTE = [[[4,5,2],[1,7,6],[2,7,4],[4,0,5],[6,0,2],[3,1,0],[2,4,6],[7,3,2],[1,7,5],[0,4,3],[3,0,2],[6,2,5],[6,5,1],[4,2,1],[1,6,2],[1,6,0],[5,1,7],[4,6,5],[7,5,3],[7,0,6],[0,5,7],[1,5,2],[0,6,5],[2,3,0],[0,3,2],[7,4,1],[4,5,7],[1,6,4],[5,2,0],[7,6,2],[3,7,2],[1,6,2],[0,4,7],[3,2,4],[1,5,3],[1,3,4],[6,4,1],[3,0,6],[3,2,1],[0,2,5],[2,1,6],[3,2,7],[1,5,2],[4,3,5],[6,1,4],[4,2,7],[1,7,3],[1,7,5],[0,1,2],[0,1,5],[2,3,6],[7,2,4],[0,1,2],[6,1,0],[0,5,7],[7,4,6],[5,7,6],[3,4,6],[1,5,2],[6,2,5],[7,6,3],[2,0,4],[1,2,5],[2,6,5],[0,7,3],[1,6,4],[5,1,7],[1,2,3],[4,5,2],[2,0,7],[6,1,3],[5,3,2],[1,3,4],[1,4,0],[4,6,3],[7,4,3],[2,1,0],[5,1,3],[7,4,0],[2,3,4],[4,5,1],[5,6,1],[1,2,3],[3,4,0],[2,5,6],[0,4,3],[1,3,2],[4,1,6],[7,5,0],[0,7,3],[5,2,0],[0,1,6],[0,7,4],[6,3,5],[4,0,6],[4,0,6],[1,6,2],[7,1,3],[3,4,6],[5,6,7],[4,5,1],[1,2,3],[1,0,6],[7,0,2],[2,7,6],[0,5,1],[7,6,2],[2,6,4],[0,2,5],[2,5,7],[3,2,7],[0,2,1],[3,5,2],[6,3,4],[0,1,2],[0,4,3],[2,1,7],[5,4,2],[7,2,3],[0,3,4],[2,7,3],[3,6,4],[2,7,1],[7,1,4],[0,7,6],[6,1,0],[3,2,4],[3,5,1],[4,6,7],[7,4,1],[6,1,7],[3,1,4],[7,4,0],[7,5,2],[1,7,2],[1,2,7],[3,2,6],[6,4,3],[0,6,1],[0,4,5],[0,1,7],[1,4,2],[0,1,2],[5,1,4],[0,1,2],[2,1,0],[1,3,6],[1,0,5],[2,1,7],[3,5,7],[2,3,1],[0,1,3],[2,5,7],[5,4,6],[3,4,5],[3,1,2],[4,2,6],[7,1,2],[5,6,1],[6,0,3],[1,5,4],[7,1,4],[6,0,4],[0,7,5],[0,7,6],[4,1,0],[7,3,2],[0,7,2],[0,3,7],[6,1,5],[3,5,4],[3,6,2],[4,1,2],[6,1,3],[6,4,0],[2,1,3],[7,4,6],[2,1,0],[2,7,3],[1,4,2],[6,7,2],[3,2,5],[7,1,4],[3,7,5],[3,4,7],[3,5,4],[4,3,5],[0,2,4],[2,7,3],[0,5,2],[6,5,3],[2,7,6],[4,2,5],[7,0,1],[0,1,7],[7,1,6],[2,3,7],[3,4,0],[5,0,3],[2,7,6],[6,0,3],[5,4,1],[6,7,4],[1,0,4],[4,0,7],[5,4,3],[3,2,6],[0,3,5],[6,5,7],[7,3,1],[6,1,4],[2,5,6],[4,2,1],[2,6,0],[4,0,5],[5,4,7],[5,3,6],[6,2,5],[6,4,0],[7,5,1],[4,1,0],[7,1,6],[7,6,2],[6,1,7],[6,3,0],[5,0,6],[6,0,1],[1,4,6],[2,7,6],[0,4,1],[3,1,5],[7,5,6],[1,7,4],[2,7,1],[0,7,4],[3,1,0],[1,6,7],[4,6,5],[3,0,6],[1,0,5],[5,0,6],[1,4,7],[2,4,6],[5,0,7],[7,0,3],[6,5,3],[6,3,2],[3,0,5],[3,7,4],[2,1,5],[1,3,0],[5,7,0],[6,2,0],[5,6,4],[7,6,0],[5,4,6],[3,7,6],[5,7,6],[5,1,7],[1,7,6],[4,3,5],[1,2,6],[6,0,1],[3,7,5],[2,0,7],[2,7,0],[0,4,5],[4,0,3],[0,5,3],[2,1,6],[3,4,1],[1,7,5],[5,1,6],[1,7,2],[6,1,0],[6,2,5],[7,6,0],[2,1,4],[3,2,7],[4,0,1],[4,2,0],[1,0,5],[5,7,6],[2,1,5],[6,5,4],[3,1,6],[6,5,7],[6,3,1],[5,7,2],[0,3,4],[4,0,6],[7,1,2],[2,5,3],[6,4,0],[6,2,3],[2,6,1],[4,5,1],[5,2,4],[1,0,3],[5,7,3],[7,2,4],[5,6,7],[1,7,3],[1,5,0],[0,3,5],[7,2,1],[6,4,0],[0,1,2],[4,2,5],[3,0,7],[0,2,4],[6,3,5],[0,5,4],[6,3,0],[5,6,1],[1,4,5],[2,6,1],[5,6,0],[2,0,6],[2,0,1],[1,3,7],[3,6,7],[2,4,6],[3,2,4],[7,1,4],[2,0,3],[3,2,6],[5,1,6],[1,4,7],[0,7,5],[5,3,6],[5,7,2],[4,0,2],[1,4,0],[2,3,4],[4,6,2],[1,2,0],[4,3,2],[4,3,7],[5,0,3],[5,3,6],[0,2,4],[1,6,3],[0,6,2],[0,6,2],[4,7,6],[5,7,3],[4,2,3],[0,7,3],[1,7,6],[3,2,5],[7,3,4],[5,7,2],[1,3,2],[6,5,7],[5,0,4],[1,4,6],[6,2,7],[3,2,4],[7,5,6],[3,4,6],[5,6,3],[5,7,0],[7,6,1],[0,7,1],[4,6,7],[0,5,2],[7,4,0],[7,4,2],[2,5,7],[5,0,1],[0,4,2],[0,1,6],[5,7,6],[6,0,1],[0,6,2],[1,6,4],[1,5,3],[0,2,6],[6,7,4],[7,2,0],[2,6,3],[6,0,3],[6,5,4],[5,7,0],[3,2,7],[1,4,7],[1,5,6],[3,7,2],[6,1,4],[1,5,4],[3,2,4],[7,2,0],[3,5,1],[2,4,6],[2,7,3],[2,4,3],[4,6,3],[4,7,0],[2,4,1],[0,3,4],[7,0,3],[5,4,1],[2,4,7],[0,7,3],[0,4,7],[7,6,4],[6,3,5],[7,3,0],[4,0,3],[4,3,7],[0,3,7],[5,7,0],[6,5,0],[1,6,0],[2,1,7],[2,1,0],[6,4,0],[0,4,5],[7,4,3],[3,2,5],[6,1,2],[4,5,3],[6,4,3],[7,3,4],[4,2,0],[3,6,1],[5,3,1],[1,0,2],[6,0,7],[4,5,2],[2,6,1],[4,0,5],[1,3,0],[2,6,5],[0,3,5],[7,1,0],[0,5,2],[3,7,1],[1,5,2],[2,5,4],[2,6,4],[0,3,4],[0,7,6],[5,4,7],[5,0,2],[2,3,0],[4,2,1],[0,7,6],[7,1,2],[6,4,2],[0,5,1],[4,6,0],[4,1,5],[7,3,0],[6,0,1],[6,3,0],[1,2,0],[1,3,0],[6,2,0],[1,4,7],[0,1,2],[4,2,3],[1,0,3],[5,0,4],[1,4,0],[4,3,1],[5,7,4],[3,5,7],[4,6,2],[6,2,5],[2,0,1],[4,0,6],[7,3,1],[0,7,6],[6,3,5],[0,4,2],[6,5,2],[0,2,5],[1,3,4],[2,6,0],[6,7,2],[2,6,0],[0,3,4],[0,6,4],[3,7,1],[7,3,0],[3,4,5],[1,0,7],[4,5,6],[5,0,3],[7,4,2],[2,1,5],[3,4,0],[4,0,6],[7,1,5],[7,3,4],[3,1,7],[5,7,6],[4,1,3],[4,1,5],[4,1,2],[3,1,4],[4,7,5],[1,0,6],[7,4,1],[0,4,2],[7,0,3],[6,4,3],[4,1,2],[3,4,6],[2,4,6]],[[5,6,1],[2,6,1],[6,5,0],[0,3,5],[5,4,6],[4,0,2],[6,2,5],[2,0,6],[1,6,0],[5,3,6],[6,3,0],[6,1,0],[1,5,7],[7,0,6],[6,2,1],[2,4,3],[1,4,0],[2,1,4],[0,6,5],[1,2,0],[3,0,1],[4,0,6],[4,0,3],[4,5,7],[2,5,1],[3,6,2],[4,1,3],[6,1,2],[5,1,3],[2,4,0],[1,4,7],[6,3,7],[0,7,4],[0,7,4],[3,1,5],[0,1,5],[5,6,7],[2,0,5],[0,7,4],[3,6,4],[0,5,1],[0,5,3],[1,6,3],[1,5,0],[1,4,3],[0,1,4],[3,0,2],[0,6,2],[4,5,7],[4,2,6],[1,4,0],[0,4,6],[1,6,3],[0,3,7],[2,6,4],[4,3,6],[0,3,6],[2,4,7],[0,5,1],[7,0,3],[4,0,6],[3,4,6],[4,5,3],[4,7,3],[7,0,2],[3,6,5],[6,5,4],[0,2,5],[5,1,7],[2,3,5],[0,7,4],[7,5,0],[2,7,5],[0,4,1],[6,4,2],[1,5,3],[6,3,1],[2,0,1],[2,1,6],[1,3,0],[2,5,7],[5,1,0],[6,5,7],[7,4,1],[6,5,7],[7,0,5],[4,6,2],[4,6,5],[0,5,2],[0,7,4],[7,5,0],[5,6,7],[5,0,4],[3,5,1],[3,4,1],[3,6,4],[2,3,0],[3,7,4],[4,7,0],[2,7,3],[7,4,6],[0,4,6],[2,1,4],[7,4,5],[0,7,5],[2,4,7],[2,4,7],[4,3,2],[2,3,1],[1,4,6],[3,4,6],[3,0,4],[0,4,3],[3,7,1],[5,3,4],[7,3,6],[0,2,1],[7,0,6],[0,2,1],[5,3,7],[7,1,0],[0,2,6],[4,5,1],[2,1,0],[6,2,5],[0,2,1],[3,0,7],[0,7,6],[2,0,4],[5,1,6],[7,3,4],[1,0,3],[2,1,6],[3,7,5],[1,4,2],[2,5,0],[2,6,3],[5,6,3],[3,2,4],[4,1,5],[3,0,1],[2,4,5],[5,7,6],[0,7,2],[5,2,6],[1,6,4],[1,4,3],[0,4,3],[3,1,2],[6,2,7],[0,4,6],[2,1,4],[4,7,2],[4,0,2],[4,1,2],[1,3,4],[1,2,0],[3,5,0],[5,4,1],[3,0,4],[6,1,5],[4,7,2],[0,4,1],[2,7,0],[6,4,7],[2,1,3],[1,7,6],[6,4,0],[4,0,7],[0,4,2],[4,1,5],[1,3,5],[7,3,0],[7,5,1],[0,1,3],[3,0,4],[2,3,5],[3,0,1],[6,3,2],[7,2,4],[2,3,5],[4,6,7],[3,5,6],[6,0,4],[3,5,0],[5,3,1],[1,5,0],[5,3,4],[0,7,4],[6,5,4],[7,6,2],[1,7,5],[1,3,4],[7,1,0],[1,4,0],[1,6,5],[4,0,5],[0,6,4],[6,2,7],[0,1,7],[1,4,6],[4,7,2],[4,1,3],[1,7,2],[2,3,7],[4,3,0],[6,0,7],[0,5,3],[6,1,3],[1,3,4],[3,7,4],[7,4,6],[5,1,2],[5,3,4],[4,2,0],[3,0,6],[6,2,0],[5,0,4],[3,2,6],[2,4,3],[3,0,5],[5,3,7],[3,5,1],[7,6,4],[5,1,7],[1,5,2],[2,5,0],[5,3,2],[2,3,7],[5,0,4],[5,3,0],[4,0,6],[7,1,4],[6,4,0],[3,5,0],[3,5,1],[2,3,7],[5,3,6],[1,2,6],[5,0,1],[2,0,7],[3,4,5],[2,6,5],[6,7,1],[1,6,3],[0,5,1],[3,0,1],[4,0,5],[7,5,0],[4,0,5],[2,6,7],[5,3,2],[6,1,7],[1,2,6],[0,4,5],[7,6,3],[0,6,2],[4,3,6],[5,2,4],[7,4,5],[3,5,4],[6,0,5],[0,7,3],[2,6,1],[3,0,6],[3,6,1],[6,4,1],[3,4,1],[4,5,0],[0,3,2],[0,5,4],[5,7,2],[1,7,4],[1,0,5],[2,7,6],[1,2,5],[1,7,5],[0,7,3],[5,3,2],[1,0,6],[5,4,2],[5,1,7],[4,2,0],[1,5,2],[2,1,4],[1,2,4],[3,0,1],[6,3,1],[2,0,5],[2,0,7],[6,5,3],[1,3,5],[2,3,4],[1,4,0],[0,5,6],[7,1,6],[0,4,1],[3,4,6],[3,5,0],[6,1,3],[0,7,6],[2,7,3],[3,2,1],[1,2,3],[4,7,0],[0,6,7],[3,2,4],[5,1,4],[6,5,0],[5,0,6],[6,1,5],[7,5,2],[7,1,5],[1,3,2],[6,4,3],[6,2,7],[1,5,3],[1,4,2],[3,7,0],[4,3,2],[2,6,5],[1,5,4],[0,7,5],[2,3,6],[7,5,4],[7,0,5],[3,5,1],[7,1,6],[7,5,6],[5,3,6],[0,3,2],[3,7,0],[0,3,5],[7,6,4],[1,7,5],[5,1,7],[6,5,1],[6,5,0],[1,2,3],[2,3,1],[2,0,3],[0,6,7],[3,7,2],[0,1,4],[1,2,7],[6,4,0],[5,2,0],[4,0,3],[2,6,0],[4,7,6],[1,4,2],[0,5,6],[1,0,4],[6,2,7],[5,2,3],[2,0,5],[2,3,1],[2,0,6],[5,3,7],[4,5,2],[1,0,4],[4,5,7],[6,0,2],[7,1,4],[4,3,0],[5,4,1],[1,0,2],[7,6,1],[6,0,1],[3,2,5],[6,0,1],[2,7,5],[0,2,7],[3,0,6],[1,4,5],[2,0,5],[4,1,6],[3,2,6],[7,0,6],[5,0,2],[2,1,4],[3,2,6],[5,7,2],[0,6,3],[5,2,1],[5,3,6],[5,2,7],[5,1,0],[1,7,6],[0,1,7],[7,1,5],[6,5,3],[0,6,7],[4,1,7],[5,2,6],[7,5,1],[5,4,3],[7,1,4],[3,0,4],[3,6,7],[7,5,2],[4,3,2],[3,7,2],[3,4,7],[4,7,6],[1,5,0],[6,3,0],[6,7,3],[5,1,7],[4,2,5],[5,3,2],[5,4,1],[2,0,3],[3,1,7],[6,1,7],[0,3,4],[1,3,7],[0,7,2],[1,2,6],[4,1,5],[2,0,6],[6,4,0],[6,1,2],[4,5,3],[5,7,6],[3,2,6],[0,7,2],[7,3,5],[7,3,1],[4,3,7],[4,1,0],[7,5,1],[7,0,1],[1,7,5],[7,3,0],[2,6,5],[1,0,5],[4,7,6],[3,7,5],[1,0,3],[3,2,5],[6,0,2],[7,1,0],[4,6,7],[1,7,2],[7,3,6],[5,4,3],[1,6,0],[1,4,2],[1,0,6],[6,5,1],[6,2,0],[6,7,5],[2,5,7],[7,2,6],[7,2,4],[6,1,4],[2,3,6],[0,6,4],[5,4,3],[5,2,7],[6,5,3],[1,5,3],[2,5,1],[5,2,4],[6,5,7],[0,1,5],[0,6,5],[5,0,7],[0,1,4],[4,7,1],[3,2,4],[2,4,3],[4,7,6],[5,2,4],[3,4,0],[6,7,4],[5,7,4],[0,2,5],[6,0,2],[2,0,6],[0,7,3],[4,5,2],[6,3,5],[5,6,1],[4,6,5],[3,5,1],[2,6,5],[0,7,6],[4,3,6],[3,7,2],[0,7,2],[5,1,6],[2,3,5],[7,4,5],[7,0,4],[6,1,0],[3,1,4],[5,3,6],[3,2,0],[6,3,1],[7,4,3],[6,5,1],[2,5,1],[2,4,1],[2,1,5],[4,3,7],[4,2,0],[0,6,3],[7,1,2],[3,5,1],[7,6,1]],[[3,5,7],[6,4,1],[3,0,1],[1,3,7],[3,0,7],[2,4,5],[7,6,0],[7,3,4],[2,7,3],[6,4,5],[0,5,3],[5,2,6],[2,0,4],[0,5,7],[1,2,6],[6,0,5],[6,0,7],[5,3,4],[7,3,1],[4,0,1],[0,6,4],[2,6,3],[4,7,3],[7,3,5],[5,6,0],[6,7,3],[1,3,7],[5,2,1],[1,2,5],[1,2,5],[7,0,4],[7,3,4],[7,6,4],[1,6,2],[3,5,6],[5,0,4],[4,6,0],[6,4,2],[5,6,0],[1,7,2],[0,5,1],[6,2,3],[0,5,7],[1,0,6],[6,7,2],[0,3,1],[2,6,5],[5,2,0],[1,7,4],[3,7,1],[5,6,7],[5,3,4],[5,0,7],[5,1,6],[1,0,3],[2,1,6],[1,7,3],[0,6,1],[0,1,4],[2,0,7],[3,7,0],[3,4,0],[1,5,6],[1,3,5],[3,0,7],[1,7,4],[1,3,2],[1,5,2],[0,4,2],[7,6,3],[1,0,3],[7,4,5],[2,7,1],[7,6,5],[1,2,4],[5,7,6],[1,2,5],[4,7,5],[5,2,3],[6,0,3],[0,4,6],[3,1,0],[4,6,7],[7,6,4],[5,0,1],[2,1,7],[3,7,6],[5,2,1],[6,2,1],[7,4,0],[4,7,2],[4,3,5],[6,5,1],[4,2,0],[1,5,6],[5,1,7],[6,7,3],[6,3,5],[4,7,1],[5,6,7],[3,0,7],[4,1,6],[1,7,3],[5,0,3],[4,6,3],[6,1,2],[1,0,4],[5,2,6],[5,7,0],[2,5,4],[0,1,5],[5,0,3],[5,3,4],[6,2,5],[2,3,7],[4,3,2],[1,3,6],[3,7,6],[7,4,3],[4,7,6],[2,0,7],[5,1,4],[0,6,7],[2,1,0],[1,5,4],[3,1,5],[0,6,7],[1,5,7],[7,5,6],[7,5,0],[0,7,3],[6,7,3],[1,3,0],[0,5,4],[5,1,2],[7,3,2],[4,5,1],[6,2,4],[2,0,6],[1,6,7],[3,5,2],[6,1,7],[4,1,7],[4,1,2],[2,1,7],[4,0,1],[3,7,0],[6,4,1],[1,3,4],[6,7,3],[7,3,5],[4,0,5],[1,5,4],[5,2,1],[3,4,1],[5,6,0],[3,5,6],[7,0,6],[4,1,7],[7,0,3],[3,4,2],[3,2,6],[2,5,4],[4,6,1],[5,3,2],[4,2,6],[4,2,3],[2,6,7],[2,7,3],[7,2,5],[7,0,5],[4,7,1],[4,2,6],[5,4,7],[3,1,4],[4,5,6],[7,3,0],[0,4,6],[4,2,6],[0,3,1],[3,2,5],[4,6,1],[3,6,5],[3,6,4],[1,0,6],[7,3,2],[4,3,5],[5,0,6],[7,6,2],[1,2,7],[4,2,1],[5,0,7],[5,4,0],[3,5,4],[4,7,3],[4,3,7],[6,1,5],[6,3,4],[7,5,1],[3,4,7],[2,6,0],[5,6,3],[0,2,1],[0,2,4],[6,7,2],[4,2,1],[5,4,2],[0,2,6],[7,1,2],[4,1,6],[0,5,4],[6,2,0],[1,4,0],[3,4,1],[0,2,1],[7,3,4],[2,0,3],[3,4,5],[5,3,0],[5,0,3],[5,6,7],[3,1,2],[1,3,7],[6,1,0],[0,6,3],[5,1,2],[5,4,3],[2,5,3],[6,1,5],[4,6,1],[7,0,2],[5,7,4],[2,1,4],[1,3,0],[7,3,5],[7,6,3],[6,7,5],[3,2,0],[0,3,1],[3,4,1],[4,6,1],[0,1,4],[3,5,1],[6,1,2],[3,7,1],[5,6,7],[2,5,0],[7,1,0],[6,3,1],[0,5,3],[7,4,2],[4,5,0],[3,2,6],[6,7,1],[4,3,2],[5,7,6],[4,5,6],[4,5,0],[6,1,2],[5,6,3],[3,6,2],[2,6,7],[3,4,0],[4,7,5],[7,6,1],[5,4,0],[4,5,0],[5,3,4],[5,1,7],[7,1,2],[1,5,3],[7,0,4],[5,6,2],[2,4,1],[3,1,4],[4,0,5],[4,6,7],[1,5,6],[0,2,5],[5,7,2],[6,3,4],[6,7,5],[1,4,6],[2,6,5],[2,5,0],[1,3,7],[0,4,2],[0,5,1],[5,4,3],[6,1,7],[1,0,7],[4,5,2],[7,4,1],[6,5,2],[7,2,6],[6,7,3],[7,4,2],[1,2,3],[6,4,0],[6,5,3],[5,1,4],[6,4,1],[2,6,1],[2,3,6],[1,5,6],[0,7,1],[2,0,4],[3,6,7],[6,3,4],[4,0,6],[0,1,6],[5,1,3],[3,5,2],[4,3,7],[5,1,3],[0,6,1],[5,4,0],[0,4,5],[1,5,3],[1,0,3],[4,2,1],[5,0,7],[6,4,0],[2,5,3],[4,6,5],[7,3,5],[4,1,6],[2,0,7],[1,5,6],[6,7,2],[6,3,1],[2,0,5],[7,5,6],[3,2,4],[2,5,4],[4,6,2],[1,0,4],[4,7,5],[4,1,0],[7,0,2],[5,3,2],[4,5,1],[6,0,5],[7,6,5],[5,1,2],[0,4,5],[3,5,2],[3,0,2],[3,2,5],[1,2,7],[2,5,4],[1,7,0],[2,5,0],[3,5,2],[7,4,3],[4,1,2],[0,2,1],[6,5,7],[4,1,7],[7,3,0],[2,3,4],[4,2,3],[2,5,3],[4,7,5],[7,2,0],[5,7,4],[5,2,6],[7,2,0],[4,3,6],[6,2,7],[6,5,1],[6,7,0],[7,5,0],[4,5,2],[2,4,7],[0,6,1],[4,1,7],[7,6,3],[1,4,6],[7,0,4],[3,4,1],[1,4,5],[2,1,4],[5,7,0],[3,4,1],[2,6,7],[4,0,3],[1,5,7],[3,6,1],[0,6,3],[2,4,1],[0,2,3],[1,7,5],[7,6,2],[3,7,6],[1,2,7],[3,6,4],[5,1,4],[3,6,7],[3,4,7],[5,6,7],[6,2,0],[7,3,5],[2,1,7],[2,4,3],[0,5,6],[5,4,7],[5,2,3],[4,2,1],[7,3,5],[4,0,5],[3,5,4],[0,2,5],[3,5,6],[2,5,3],[4,1,3],[7,4,3],[7,4,5],[4,1,2],[0,7,3],[1,2,3],[1,0,3],[0,7,4],[0,1,6],[1,6,2],[6,1,7],[6,4,7],[3,7,6],[6,0,2],[7,2,6],[7,4,1],[7,0,1],[0,1,7],[6,7,0],[6,1,5],[0,3,7],[0,6,5],[4,1,7],[4,6,0],[6,1,7],[0,4,1],[6,7,1],[6,3,7],[6,1,7],[7,3,2],[1,7,3],[7,5,1],[5,1,2],[5,0,3],[0,6,1],[2,7,4],[1,0,3],[1,3,5],[1,2,3],[4,2,7],[7,6,3],[2,5,7],[4,5,3],[5,6,0],[2,3,7],[6,2,7],[3,4,7],[2,6,3],[0,1,2],[5,1,2],[7,4,6],[3,5,4],[3,1,5],[1,7,6],[1,0,4],[5,0,1],[6,1,2],[5,2,0],[3,6,1],[0,6,5],[4,6,7],[5,2,3],[1,4,2],[2,5,4],[4,6,2],[4,3,6],[0,1,6],[4,7,5],[7,2,1],[7,2,6],[3,2,6],[1,6,2],[5,3,4],[5,0,3],[7,3,2],[5,6,7],[2,1,5],[6,5,2],[0,5,6],[0,3,6],[2,0,4],[4,7,5],[4,6,5],[3,5,4],[7,3,1],[1,3,2],[1,2,5],[0,4,3],[0,5,6],[5,0,1],[5,7,3],[0,2,1],[6,3,5],[1,5,4],[0,7,2],[4,0,5],[7,0,6]],[[0,6,4],[2,1,6],[1,2,6],[5,0,6],[0,3,7],[7,5,3],[0,7,1],[5,1,3],[0,1,5],[3,4,2],[5,0,6],[6,4,0],[7,3,2],[7,2,3],[2,1,0],[4,2,1],[0,2,5],[3,4,5],[4,6,2],[7,2,6],[4,0,2],[5,2,1],[7,2,1],[1,7,3],[3,5,6],[4,1,0],[1,3,2],[2,6,7],[5,4,2],[0,1,5],[1,0,6],[0,5,2],[1,2,6],[1,5,3],[1,6,5],[7,5,4],[2,0,3],[4,0,3],[0,6,1],[4,1,5],[6,2,4],[3,2,1],[5,3,1],[5,7,1],[5,6,0],[7,0,5],[0,6,4],[2,4,6],[5,1,2],[7,1,2],[0,4,7],[5,3,1],[4,6,2],[1,4,3],[6,7,0],[6,7,1],[0,1,4],[1,6,4],[3,2,7],[7,2,0],[5,4,7],[4,2,7],[5,2,0],[6,7,3],[5,0,6],[6,7,0],[3,4,5],[4,7,0],[0,5,4],[5,6,4],[7,6,2],[4,7,2],[0,7,4],[1,2,6],[6,5,7],[7,4,2],[7,6,0],[3,6,4],[7,4,0],[4,3,2],[2,3,7],[6,4,1],[0,4,5],[0,7,5],[6,0,7],[6,5,3],[3,1,0],[7,2,0],[2,6,5],[0,1,4],[0,6,3],[7,2,1],[7,6,5],[5,6,3],[5,1,3],[1,4,7],[6,4,1],[2,3,0],[1,6,7],[5,2,6],[0,1,5],[0,3,2],[5,4,0],[1,2,4],[5,3,1],[6,3,2],[3,2,4],[4,0,1],[4,6,0],[7,5,0],[7,2,0],[4,2,5],[3,6,4],[7,6,2],[7,3,2],[7,0,2],[4,1,7],[1,5,7],[6,1,4],[6,2,0],[5,6,7],[2,6,0],[6,3,4],[7,6,1],[1,7,5],[6,2,0],[5,0,4],[5,1,7],[4,3,0],[7,5,1],[3,1,6],[7,2,5],[3,2,6],[4,5,7],[1,4,2],[3,0,7],[1,7,3],[7,5,3],[3,0,7],[7,2,4],[1,5,7],[1,3,4],[4,7,0],[7,4,3],[2,4,6],[2,5,3],[3,4,0],[0,5,2],[5,2,1],[4,5,6],[6,0,1],[0,2,4],[1,7,3],[1,5,7],[7,1,3],[6,1,4],[2,1,5],[1,7,3],[7,5,3],[5,2,1],[2,6,0],[5,7,0],[1,5,0],[5,2,0],[4,1,6],[1,2,0],[0,4,3],[2,3,7],[3,0,6],[4,1,5],[4,2,0],[7,6,5],[5,0,3],[4,7,2],[1,0,4],[2,7,1],[6,0,2],[5,0,1],[1,0,7],[4,0,2],[0,7,1],[7,0,2],[5,4,2],[4,5,7],[7,1,4],[2,7,6],[2,7,5],[2,4,0],[2,6,0],[2,6,7],[7,2,6],[2,7,6],[5,4,2],[2,0,4],[6,3,0],[0,5,6],[1,0,3],[1,7,2],[0,6,2],[7,0,4],[7,6,1],[7,3,4],[2,5,4],[3,2,6],[7,0,5],[6,1,4],[5,6,4],[0,3,4],[1,0,7],[3,2,6],[2,5,0],[1,3,5],[3,0,6],[3,0,1],[0,3,7],[5,3,2],[0,6,3],[0,2,5],[4,1,0],[3,1,5],[5,6,3],[6,3,2],[2,4,5],[4,3,1],[7,6,3],[3,4,7],[0,7,1],[3,0,4],[5,2,0],[2,7,5],[6,1,4],[2,3,6],[3,5,2],[5,7,4],[4,0,6],[6,0,3],[1,5,4],[4,7,5],[3,2,1],[4,3,5],[0,4,5],[2,0,7],[7,4,5],[6,5,2],[6,5,1],[0,6,4],[4,1,3],[5,3,1],[0,3,7],[5,4,1],[0,2,6],[6,1,0],[4,1,6],[6,0,2],[2,3,5],[7,1,2],[7,5,4],[3,0,4],[2,4,7],[0,1,2],[7,0,3],[4,5,0],[3,5,4],[3,1,2],[2,7,4],[4,5,7],[0,1,5],[4,7,1],[6,7,5],[2,1,5],[1,3,0],[5,6,3],[3,7,5],[2,0,6],[0,3,4],[4,1,5],[5,1,6],[3,2,7],[3,0,1],[0,4,1],[2,7,1],[2,6,7],[4,7,1],[2,3,7],[7,2,5],[1,4,0],[6,2,0],[5,4,6],[6,3,0],[3,2,4],[3,2,4],[1,5,7],[4,0,5],[6,3,1],[2,4,0],[5,1,7],[7,5,2],[4,2,3],[4,1,7],[4,2,3],[0,4,7],[2,3,1],[6,7,2],[1,0,2],[4,6,1],[6,2,0],[6,7,0],[7,1,3],[4,0,3],[5,0,6],[2,0,7],[1,6,2],[1,5,6],[7,3,2],[3,0,4],[0,4,2],[1,7,6],[1,7,2],[7,1,6],[5,2,6],[7,0,2],[3,2,6],[4,0,2],[3,7,1],[4,0,3],[6,7,3],[6,4,7],[0,2,7],[6,7,4],[4,3,0],[0,1,5],[2,5,6],[7,6,2],[6,5,3],[1,7,2],[2,7,5],[6,4,1],[3,6,2],[0,1,4],[1,3,7],[7,0,4],[3,6,1],[4,5,6],[0,5,1],[3,6,5],[6,3,0],[5,4,6],[7,6,2],[7,3,1],[7,5,3],[3,0,1],[0,6,7],[3,7,0],[3,0,7],[0,4,5],[0,4,1],[0,6,5],[6,2,5],[6,5,7],[4,6,2],[1,5,6],[4,6,1],[7,3,2],[5,0,2],[3,5,2],[0,5,1],[6,4,1],[0,5,2],[6,0,1],[2,5,0],[1,2,3],[1,5,2],[7,1,0],[6,1,3],[1,6,2],[5,3,6],[0,1,2],[4,5,1],[2,4,5],[2,7,1],[2,7,3],[1,2,7],[0,4,3],[5,7,1],[6,2,5],[3,1,5],[0,1,5],[1,6,7],[0,2,1],[1,6,5],[0,7,6],[1,6,2],[5,4,3],[2,5,7],[5,2,7],[7,4,3],[7,4,0],[1,5,6],[2,6,7],[1,4,2],[7,6,1],[6,4,1],[0,2,5],[6,1,0],[7,0,1],[0,5,7],[4,2,0],[1,2,6],[2,4,6],[5,3,2],[5,4,3],[6,7,3],[5,0,4],[6,0,3],[0,4,1],[0,3,7],[3,0,6],[4,7,0],[0,3,6],[3,2,7],[0,3,5],[3,1,4],[5,0,6],[5,4,6],[2,7,4],[4,6,7],[6,2,3],[6,2,1],[7,3,0],[0,1,6],[4,7,5],[0,7,5],[2,5,0],[4,5,2],[0,2,6],[3,1,5],[6,1,2],[0,7,5],[5,4,0],[1,2,0],[5,7,0],[2,7,0],[1,3,7],[0,5,7],[2,0,3],[1,0,7],[5,4,6],[0,7,5],[2,5,6],[7,5,4],[0,1,4],[2,0,5],[1,5,0],[5,3,0],[6,7,3],[0,4,1],[2,6,4],[7,3,0],[0,4,7],[5,7,2],[0,4,3],[0,4,2],[4,7,3],[2,5,4],[7,6,1],[5,1,7],[3,1,2],[0,5,3],[3,6,4],[4,7,0],[2,6,7],[7,1,6],[5,0,7],[6,1,7],[1,2,6],[2,7,1],[2,4,7],[2,7,0],[7,2,3],[5,4,1],[5,1,0],[1,2,6],[5,6,1],[4,0,6],[4,2,3],[3,0,1],[1,3,0],[3,5,1],[0,7,3],[0,2,1],[5,7,6],[7,0,2],[7,2,4],[5,1,3],[7,3,5],[3,2,1],[6,7,2],[7,6,4],[5,4,1],[2,1,4],[0,2,4],[2,6,1],[4,0,6],[4,3,5],[3,6,0],[1,7,4],[2,4,0],[6,0,5],[4,2,0],[4,1,2],[1,4,2],[4,1,0]],[[1,3,5],[1,2,6],[4,5,6],[7,6,0],[1,2,7],[4,0,5],[6,1,3],[6,1,7],[6,1,2],[2,4,5],[3,1,4],[1,3,4],[4,5,2],[7,5,4],[0,6,5],[1,2,3],[7,4,0],[1,3,0],[7,4,0],[0,5,1],[1,2,4],[4,5,7],[4,0,3],[3,4,5],[5,3,6],[2,0,7],[1,7,0],[0,3,4],[1,7,5],[6,4,2],[1,7,2],[2,0,6],[0,4,3],[6,4,2],[1,3,5],[3,5,2],[4,6,1],[7,3,5],[2,5,3],[1,6,0],[5,2,7],[6,7,2],[4,7,5],[2,5,3],[6,7,0],[0,5,2],[6,4,1],[1,5,3],[2,4,0],[7,0,5],[4,1,3],[6,2,4],[5,4,1],[3,5,7],[5,1,2],[3,2,0],[7,6,2],[0,1,6],[0,2,1],[3,2,4],[2,0,7],[1,4,3],[0,1,7],[5,2,6],[2,3,5],[1,0,3],[0,4,2],[5,6,1],[2,6,7],[2,4,6],[3,2,0],[3,2,7],[4,7,2],[4,6,0],[7,5,0],[5,3,1],[6,1,2],[4,5,6],[4,3,5],[5,1,7],[4,1,5],[6,5,4],[0,5,7],[5,6,3],[0,1,2],[0,2,7],[1,7,3],[6,5,4],[5,7,3],[4,6,2],[4,3,2],[1,7,5],[2,7,4],[1,3,0],[1,6,0],[2,5,7],[6,5,0],[3,5,7],[1,3,4],[5,2,7],[5,3,4],[4,6,0],[3,4,7],[1,5,3],[0,1,2],[4,6,2],[7,4,3],[0,2,7],[3,7,2],[5,7,1],[0,4,3],[1,4,6],[7,3,2],[3,1,4],[5,3,2],[2,6,1],[0,4,2],[5,1,6],[5,6,4],[6,4,3],[3,5,6],[5,1,6],[3,4,5],[2,3,6],[5,2,6],[1,7,3],[7,0,3],[5,3,0],[2,7,3],[4,2,0],[3,5,0],[1,7,3],[6,2,4],[4,0,7],[2,1,4],[1,2,4],[6,1,0],[5,7,4],[1,4,2],[7,6,2],[4,0,7],[7,3,0],[1,5,6],[2,3,6],[1,7,3],[5,3,4],[2,4,5],[5,6,0],[4,3,5],[2,1,3],[1,3,5],[2,4,3],[4,2,1],[4,3,7],[6,1,5],[5,0,1],[4,7,3],[1,5,4],[6,2,7],[3,2,0],[3,0,2],[7,5,4],[7,0,3],[7,0,2],[0,7,5],[3,7,1],[6,3,4],[0,2,7],[7,5,1],[1,2,3],[1,0,7],[1,2,5],[1,5,7],[5,6,1],[7,3,6],[6,4,5],[1,2,3],[7,5,4],[7,4,3],[1,3,0],[7,0,3],[6,5,1],[1,7,6],[3,4,6],[7,5,3],[6,4,1],[5,0,1],[2,6,1],[4,2,0],[6,4,2],[6,5,4],[2,7,1],[0,2,5],[0,2,1],[2,1,3],[6,7,3],[3,1,7],[7,2,4],[3,5,6],[0,4,7],[5,3,2],[0,2,5],[6,7,5],[4,7,2],[0,4,7],[2,5,1],[1,4,3],[2,5,7],[2,7,6],[7,2,3],[0,7,4],[2,1,7],[1,6,7],[1,5,6],[5,4,6],[2,1,6],[1,5,6],[5,1,7],[3,2,4],[7,0,2],[7,2,4],[6,4,5],[3,2,6],[0,1,3],[2,4,1],[5,2,0],[4,3,0],[5,0,7],[1,5,4],[4,3,6],[6,1,7],[1,6,4],[7,4,3],[3,7,2],[2,4,0],[0,7,2],[0,2,5],[0,1,7],[6,7,4],[3,1,2],[3,2,6],[3,6,0],[6,4,0],[6,0,3],[5,7,0],[2,0,1],[2,7,5],[7,3,4],[6,3,1],[4,1,2],[4,6,5],[2,3,0],[0,2,6],[4,7,5],[3,4,1],[1,6,2],[4,3,0],[0,6,2],[3,4,7],[6,2,0],[6,5,0],[2,6,1],[5,4,6],[5,0,2],[6,7,1],[6,0,1],[5,2,4],[7,3,6],[5,2,4],[0,6,2],[0,2,5],[0,3,1],[4,7,2],[1,5,7],[4,3,7],[7,1,4],[2,1,3],[0,1,6],[1,6,0],[1,0,5],[6,2,3],[6,0,3],[7,5,4],[5,4,2],[2,4,1],[3,7,5],[0,2,5],[2,3,0],[3,4,7],[2,4,6],[7,5,0],[2,7,5],[4,0,6],[0,7,5],[0,6,4],[6,3,1],[6,3,7],[7,5,2],[0,6,2],[2,4,7],[4,5,6],[2,0,3],[0,7,1],[6,0,3],[2,1,0],[3,5,2],[7,1,2],[1,7,4],[1,4,2],[0,4,7],[4,5,7],[2,6,3],[2,6,1],[6,5,7],[2,5,6],[2,4,6],[5,2,4],[4,2,6],[4,6,7],[3,0,7],[2,1,6],[4,5,0],[0,7,4],[2,3,7],[6,2,5],[0,6,4],[5,1,2],[5,0,2],[7,6,0],[6,1,4],[1,3,7],[6,3,1],[1,2,3],[1,4,3],[0,4,3],[5,4,3],[1,5,0],[7,4,2],[2,7,0],[5,0,4],[1,6,0],[6,2,0],[2,4,5],[5,3,4],[7,5,6],[2,5,7],[4,2,1],[3,5,7],[1,0,5],[5,1,4],[6,3,1],[0,2,3],[5,3,4],[1,7,6],[0,5,4],[5,7,1],[4,5,3],[0,7,1],[7,6,4],[3,2,5],[5,4,1],[5,3,7],[7,0,1],[6,7,1],[4,2,5],[3,0,1],[4,6,2],[4,0,6],[6,3,2],[4,0,1],[7,6,0],[2,5,1],[7,2,4],[3,4,7],[0,1,7],[2,7,4],[0,3,6],[0,4,3],[2,7,5],[4,5,7],[1,0,3],[3,5,7],[3,2,5],[2,6,7],[2,4,7],[4,5,2],[2,3,0],[5,1,3],[1,2,6],[5,2,6],[5,2,6],[4,2,6],[7,4,1],[1,3,6],[0,5,7],[7,2,5],[6,0,5],[6,1,7],[4,3,2],[7,6,1],[2,5,0],[5,6,4],[0,5,1],[1,6,0],[2,4,3],[5,2,4],[1,0,4],[1,6,5],[3,5,1],[6,7,4],[3,0,5],[0,1,4],[0,7,5],[2,1,3],[7,5,6],[6,5,7],[2,0,6],[7,5,2],[0,7,1],[2,4,6],[3,4,2],[6,4,1],[7,4,1],[7,3,5],[7,0,5],[5,1,3],[3,7,6],[7,1,4],[4,7,5],[4,1,7],[5,1,0],[6,1,5],[4,2,1],[5,7,4],[5,6,7],[2,1,0],[4,5,0],[7,0,2],[6,2,5],[6,2,1],[7,4,3],[5,0,3],[2,7,5],[5,4,2],[2,0,7],[5,6,3],[4,0,7],[0,6,4],[3,0,2],[6,1,2],[3,1,2],[0,4,1],[3,2,1],[2,6,5],[0,1,6],[5,7,6],[1,6,5],[0,7,5],[2,6,5],[4,5,7],[3,6,5],[3,5,0],[5,7,3],[7,3,2],[7,6,1],[3,7,6],[4,7,0],[3,7,4],[4,1,6],[6,3,1],[7,1,3],[5,6,1],[2,7,3],[7,3,4],[2,4,5],[0,1,3],[3,2,4],[0,3,4],[3,7,5],[2,1,3],[0,1,4],[3,7,0],[0,6,4],[0,5,4],[1,7,4],[5,1,2],[6,4,3],[4,7,0],[2,0,4],[0,5,4],[1,7,6],[5,3,1],[5,0,3],[5,3,4],[0,7,1],[1,7,4],[7,0,3],[1,7,3],[3,7,5],[2,6,5],[5,6,0],[4,0,2],[1,6,5],[5,0,1],[2,0,6],[5,1,7],[0,3,6],[0,2,7],[2,5,6],[0,3,1],[3,1,4],[0,7,4]],[[5,0,2],[4,6,1],[4,5,2],[6,3,5],[0,1,2],[7,6,2],[2,1,0],[2,4,3],[0,5,6],[0,2,6],[4,2,7],[4,3,5],[7,2,0],[1,4,2],[6,1,0],[6,0,3],[2,1,0],[6,7,1],[4,1,6],[4,5,6],[3,4,2],[3,0,5],[0,1,6],[5,6,7],[5,7,0],[1,4,0],[5,0,7],[4,3,2],[2,7,5],[7,2,1],[6,3,2],[1,7,4],[1,3,2],[4,1,3],[5,6,4],[6,2,3],[0,4,6],[6,0,5],[4,7,1],[3,1,0],[0,3,7],[0,4,3],[7,4,3],[7,5,4],[5,1,7],[4,7,0],[3,5,7],[7,3,6],[5,7,3],[6,4,7],[2,1,5],[7,0,2],[5,0,4],[7,4,3],[1,6,3],[7,5,0],[1,0,5],[0,3,1],[2,7,0],[2,3,4],[1,3,4],[7,6,1],[4,1,0],[1,5,0],[4,0,2],[4,6,1],[3,1,4],[7,1,6],[3,1,0],[5,1,3],[6,2,7],[0,1,7],[1,6,7],[3,4,6],[6,3,5],[6,1,3],[1,2,4],[2,7,6],[1,5,2],[7,2,5],[7,5,1],[5,3,6],[3,5,4],[3,4,1],[7,0,3],[6,1,5],[4,6,1],[3,2,4],[5,2,1],[4,6,7],[7,2,5],[4,3,2],[1,0,7],[5,2,1],[0,2,5],[6,2,1],[7,6,4],[5,0,4],[4,3,1],[6,1,3],[7,2,4],[3,6,1],[0,4,6],[4,3,7],[1,5,2],[1,2,6],[6,7,5],[5,2,4],[6,1,5],[2,3,6],[3,0,1],[4,3,0],[1,2,7],[0,2,6],[6,1,0],[6,4,7],[0,4,6],[1,0,5],[2,4,3],[0,7,1],[2,5,7],[1,5,7],[7,4,0],[7,3,5],[6,3,2],[6,3,2],[5,1,6],[4,6,3],[5,3,1],[3,5,2],[6,0,3],[3,1,7],[0,4,3],[2,4,1],[2,6,5],[4,2,5],[4,2,7],[0,6,5],[5,3,6],[4,5,7],[2,4,1],[4,0,6],[5,1,7],[0,3,6],[2,0,1],[3,4,0],[1,0,3],[6,1,7],[0,4,1],[6,4,0],[6,1,4],[5,7,4],[3,7,0],[3,5,4],[1,5,0],[0,3,1],[5,2,0],[1,7,5],[0,6,3],[2,4,1],[7,5,2],[6,7,4],[5,4,0],[3,6,0],[5,6,1],[4,0,2],[1,6,0],[3,6,0],[1,6,3],[2,3,5],[1,2,6],[0,4,7],[2,6,7],[1,4,7],[5,7,1],[2,3,0],[1,7,4],[6,4,1],[3,7,6],[1,6,3],[2,5,4],[4,5,0],[3,2,0],[7,0,1],[6,3,1],[3,2,1],[4,6,3],[3,5,6],[0,7,4],[1,4,0],[7,4,5],[7,4,0],[3,4,7],[5,1,2],[1,3,6],[6,4,3],[3,6,5],[2,3,0],[6,2,1],[6,0,3],[7,1,4],[7,4,6],[6,5,4],[4,6,2],[0,3,5],[4,5,0],[2,3,4],[1,6,2],[1,3,5],[1,2,3],[3,0,6],[5,4,7],[7,2,6],[7,0,1],[4,6,5],[0,2,6],[7,5,6],[0,1,6],[5,4,6],[2,1,6],[4,1,5],[6,3,4],[3,2,5],[6,0,3],[5,1,0],[4,6,2],[0,6,3],[1,6,3],[5,0,2],[2,5,0],[2,3,5],[6,2,5],[2,1,5],[2,6,7],[1,3,6],[2,6,4],[1,0,7],[3,4,5],[1,0,4],[6,1,3],[7,1,5],[7,1,4],[4,3,6],[5,1,7],[2,4,5],[3,2,1],[7,3,5],[1,2,3],[1,3,7],[3,2,7],[2,5,0],[5,1,3],[3,0,5],[3,6,1],[5,1,6],[5,4,3],[3,2,5],[6,3,5],[2,5,6],[6,0,3],[3,7,2],[1,0,6],[6,0,3],[2,5,6],[6,4,2],[2,7,1],[4,2,7],[7,3,1],[6,7,3],[0,4,7],[3,6,7],[0,4,5],[6,0,7],[3,7,2],[0,4,2],[7,6,2],[0,1,5],[6,7,4],[4,6,1],[2,6,7],[3,1,6],[5,0,7],[6,3,0],[7,4,1],[0,5,3],[5,4,3],[7,5,6],[4,6,3],[2,6,4],[7,3,5],[1,3,2],[3,4,2],[0,6,3],[2,0,1],[2,6,7],[4,6,7],[0,3,6],[0,1,5],[6,7,3],[5,7,0],[5,4,6],[1,4,7],[7,4,1],[1,4,6],[1,5,6],[4,3,5],[5,4,1],[1,4,2],[5,6,4],[1,5,0],[4,6,3],[7,2,1],[7,3,2],[6,3,0],[2,1,0],[3,7,6],[4,7,2],[6,1,3],[2,1,3],[6,0,4],[6,4,5],[1,5,2],[6,5,7],[0,4,5],[7,6,1],[0,3,1],[6,4,5],[1,0,6],[1,7,5],[7,5,0],[3,7,0],[4,0,1],[1,3,5],[3,2,1],[7,0,4],[4,0,7],[1,2,0],[4,1,7],[6,1,5],[1,3,6],[7,2,4],[5,1,6],[6,2,5],[5,1,3],[2,5,4],[6,5,4],[0,4,6],[7,1,0],[4,7,0],[3,0,5],[6,7,5],[6,0,4],[1,5,7],[5,2,6],[7,5,0],[7,0,5],[2,5,4],[0,7,3],[0,4,3],[0,6,3],[0,2,1],[6,5,0],[6,0,3],[3,6,4],[6,7,2],[0,3,6],[5,2,6],[3,5,6],[5,3,0],[4,5,2],[3,1,5],[6,2,1],[2,5,3],[2,6,0],[2,6,1],[5,6,4],[7,2,6],[1,4,7],[5,2,1],[6,2,1],[2,5,0],[6,0,5],[0,5,1],[6,5,4],[1,2,6],[2,6,5],[3,1,7],[0,1,3],[7,4,5],[0,1,3],[6,2,0],[4,0,3],[2,5,0],[1,6,3],[3,6,4],[5,1,6],[7,0,1],[3,2,6],[7,0,4],[7,0,1],[4,0,6],[2,6,5],[3,1,5],[0,1,6],[2,6,3],[6,0,3],[1,3,5],[1,3,6],[0,1,7],[4,7,5],[1,2,3],[7,2,6],[4,5,1],[3,2,7],[0,4,1],[1,0,2],[3,6,7],[5,7,3],[7,1,6],[0,7,6],[6,2,3],[3,5,7],[4,0,6],[4,3,6],[7,2,0],[5,7,1],[6,3,2],[3,2,0],[3,2,0],[6,4,2],[6,7,2],[4,2,1],[4,2,6],[1,5,0],[3,0,6],[6,4,1],[4,1,0],[2,0,7],[1,6,0],[5,0,3],[7,6,0],[2,7,0],[1,0,3],[5,0,3],[4,5,0],[5,1,6],[6,1,0],[1,0,5],[2,6,3],[2,4,0],[6,0,5],[5,7,6],[5,4,3],[5,4,0],[1,2,3],[1,6,4],[2,7,4],[3,7,5],[6,5,1],[2,3,4],[7,0,6],[2,4,3],[0,3,2],[7,1,2],[4,2,6],[7,3,6],[6,0,3],[3,5,6],[6,2,3],[5,6,1],[7,5,6],[4,0,1],[5,0,3],[7,1,3],[1,0,6],[0,2,5],[0,6,4],[7,0,6],[5,2,0],[7,2,5],[1,7,6],[2,5,0],[3,2,7],[2,4,0],[6,4,0],[6,5,4],[4,0,2],[0,2,7],[3,1,5],[0,2,1],[2,1,4],[7,6,3],[2,4,5],[5,3,7],[6,0,2],[5,1,0],[7,4,1],[4,0,1],[2,6,1],[0,6,4],[4,0,5],[2,1,0],[5,1,6],[1,7,5],[5,0,7],[2,0,3],[5,3,6],[0,5,4],[6,7,5],[2,4,6],[3,5,1],[7,0,5]],[[7,1,2],[4,3,0],[5,3,7],[3,6,4],[0,5,6],[7,4,0],[1,5,4],[4,1,7],[5,3,0],[5,0,1],[0,7,3],[1,2,6],[0,1,2],[1,2,7],[0,2,6],[0,7,4],[4,3,0],[3,2,1],[1,0,3],[7,4,6],[2,0,3],[7,4,5],[3,4,5],[1,7,6],[3,0,1],[0,4,2],[3,4,7],[1,5,7],[3,1,4],[5,2,3],[6,4,1],[0,5,4],[3,4,1],[5,0,6],[3,5,7],[2,5,0],[2,5,1],[7,4,6],[5,4,2],[2,0,3],[6,0,5],[6,5,4],[2,4,6],[1,4,5],[5,4,3],[7,2,0],[3,1,6],[7,5,2],[0,2,5],[5,3,7],[5,6,0],[7,3,0],[5,1,3],[7,6,1],[2,5,4],[1,7,4],[2,0,4],[3,4,0],[1,3,6],[4,1,7],[2,1,3],[5,4,1],[3,0,6],[7,1,6],[6,2,5],[6,3,0],[4,0,6],[1,4,0],[6,5,3],[2,3,7],[1,5,3],[5,1,4],[5,6,2],[7,6,5],[3,2,5],[1,7,2],[2,4,3],[3,1,4],[5,2,6],[4,1,0],[2,7,1],[5,3,1],[0,2,7],[6,3,7],[1,7,5],[4,2,6],[4,0,3],[7,1,0],[2,3,1],[6,7,0],[4,5,3],[5,3,7],[3,4,1],[6,1,5],[3,0,1],[4,0,2],[6,7,4],[4,0,7],[7,6,1],[5,2,1],[6,2,4],[2,7,0],[0,7,1],[0,6,2],[3,1,5],[2,1,4],[2,7,6],[3,7,1],[6,1,0],[5,1,6],[3,7,6],[7,0,4],[5,3,4],[6,2,3],[0,6,2],[4,2,3],[3,5,2],[5,6,0],[3,2,7],[4,2,0],[6,0,3],[7,6,4],[0,4,3],[6,0,1],[6,7,3],[4,6,1],[3,6,4],[3,4,1],[0,7,3],[6,4,0],[1,0,6],[5,3,4],[2,5,1],[4,3,6],[2,1,5],[4,7,0],[0,5,6],[7,5,6],[3,0,1],[0,5,2],[4,3,6],[7,1,6],[4,6,5],[0,1,7],[0,5,7],[5,7,3],[3,4,0],[3,1,2],[7,0,2],[7,3,4],[3,6,0],[2,6,3],[6,1,5],[2,3,7],[7,1,2],[4,5,7],[2,4,6],[5,7,6],[2,4,6],[1,5,6],[4,7,2],[5,4,7],[0,7,3],[4,6,0],[1,2,4],[5,7,6],[0,3,6],[6,4,3],[0,5,7],[3,2,6],[7,2,5],[0,7,3],[2,7,4],[6,5,7],[5,1,6],[0,7,5],[0,4,3],[0,5,3],[6,2,1],[0,5,7],[4,3,5],[4,0,6],[6,1,2],[1,6,7],[3,1,7],[7,4,1],[2,6,3],[3,1,5],[2,7,4],[0,3,2],[3,1,5],[4,1,7],[3,7,5],[3,4,2],[0,6,2],[7,1,4],[3,2,4],[1,0,5],[2,1,4],[3,7,2],[6,2,3],[0,6,4],[6,0,4],[4,0,6],[2,5,6],[3,4,6],[7,2,6],[7,0,5],[6,4,2],[6,5,1],[6,2,5],[5,2,4],[7,1,3],[6,4,7],[0,1,4],[0,4,3],[0,2,6],[1,7,3],[6,2,3],[2,4,0],[3,0,7],[0,5,3],[5,2,3],[2,4,0],[2,0,5],[2,0,3],[1,0,2],[0,6,4],[6,3,0],[2,5,7],[5,4,7],[5,1,4],[1,2,4],[1,6,4],[1,4,6],[7,3,4],[6,3,2],[0,5,1],[5,3,7],[6,2,0],[6,3,7],[4,6,5],[5,3,4],[7,0,3],[6,4,5],[1,2,7],[3,1,4],[7,1,4],[6,3,1],[2,1,7],[1,5,2],[5,3,4],[3,1,2],[5,4,6],[5,6,4],[0,1,3],[2,0,6],[0,5,2],[4,2,3],[0,6,7],[1,4,3],[1,3,7],[1,7,4],[4,3,7],[0,4,3],[4,1,7],[6,4,5],[1,3,4],[4,0,2],[1,3,2],[1,4,6],[0,6,1],[7,6,5],[6,4,2],[2,0,5],[2,6,1],[4,2,6],[0,5,4],[7,6,0],[3,0,5],[5,3,1],[4,3,5],[3,6,1],[3,4,0],[0,6,4],[7,1,0],[7,1,5],[4,5,7],[2,0,6],[3,4,6],[4,2,7],[0,7,2],[1,4,7],[2,5,3],[1,7,6],[3,7,0],[5,7,2],[4,1,2],[0,2,4],[6,2,1],[3,7,4],[3,1,7],[2,3,1],[5,7,4],[4,7,2],[6,5,3],[3,6,4],[4,0,6],[3,7,1],[3,6,2],[4,2,7],[7,2,4],[6,3,5],[0,5,1],[6,7,1],[4,0,1],[3,4,0],[0,6,3],[4,5,2],[5,7,3],[3,5,0],[1,0,4],[1,5,7],[4,7,2],[5,4,7],[6,3,5],[0,7,3],[3,4,1],[1,0,7],[6,0,1],[4,0,3],[5,6,3],[2,0,7],[5,4,0],[0,5,3],[4,1,5],[7,1,4],[1,2,6],[2,5,0],[2,4,3],[1,5,0],[2,4,5],[0,3,4],[4,2,3],[5,6,2],[5,0,1],[2,3,7],[0,4,5],[1,5,7],[4,7,2],[5,4,1],[4,2,7],[4,2,6],[6,0,3],[0,6,2],[4,6,7],[2,0,1],[4,6,2],[3,4,2],[0,5,2],[3,1,2],[2,3,1],[0,5,4],[0,2,6],[4,6,7],[0,3,1],[6,5,3],[6,3,5],[1,4,0],[7,5,1],[1,6,7],[4,1,6],[1,0,7],[3,6,2],[1,6,3],[7,0,5],[7,4,5],[0,6,1],[6,5,2],[3,0,7],[6,7,0],[2,3,7],[6,4,7],[4,7,0],[6,3,2],[7,1,2],[1,7,5],[0,5,1],[4,3,7],[2,7,3],[3,0,6],[3,2,5],[2,0,6],[5,2,4],[7,6,0],[0,1,2],[0,6,1],[0,7,5],[0,3,1],[7,3,5],[1,3,2],[7,5,4],[6,4,0],[7,5,1],[0,5,2],[6,4,2],[1,4,5],[4,0,6],[4,6,1],[1,7,5],[6,2,7],[7,3,4],[4,0,2],[4,5,2],[5,7,2],[3,4,1],[0,2,4],[1,6,5],[5,2,0],[5,3,0],[3,6,0],[6,0,1],[4,7,3],[3,0,2],[6,2,7],[3,6,7],[6,1,2],[6,1,4],[5,7,4],[1,7,0],[7,2,1],[6,4,7],[5,0,3],[5,3,7],[2,1,5],[7,0,2],[1,4,7],[6,4,0],[5,3,7],[6,4,7],[3,1,7],[4,5,7],[2,7,3],[1,2,4],[0,7,5],[6,1,7],[7,2,4],[1,4,0],[3,5,6],[4,5,1],[1,5,7],[5,6,4],[5,4,6],[0,4,7],[5,3,0],[7,0,1],[0,4,6],[4,2,1],[0,5,7],[6,1,2],[4,2,5],[4,3,2],[7,6,2],[5,3,2],[7,2,5],[6,0,7],[7,1,4],[0,2,3],[5,4,6],[3,5,7],[5,4,2],[5,6,7],[4,7,5],[7,3,1],[7,5,4],[1,3,6],[0,2,1],[4,2,0],[6,4,0],[7,0,2],[3,4,7],[4,1,6],[2,3,6],[5,7,6],[3,7,6],[0,5,4],[5,0,3],[4,5,3],[5,3,6],[7,5,4],[2,6,7],[1,3,7],[3,4,2],[6,1,5],[1,7,6],[4,1,5],[6,2,3],[2,5,4],[5,0,6],[6,1,3],[6,3,7],[5,0,1],[2,4,7],[6,4,5],[0,5,4],[2,0,1],[5,3,4],[0,4,7],[2,6,0],[2,1,3],[1,0,2],[7,1,5]],[[5,1,0],[2,4,1],[1,6,5],[6,3,2],[2,7,0],[1,6,3],[3,6,0],[4,6,0],[3,7,1],[3,2,5],[0,4,6],[7,1,2],[5,2,6],[4,3,2],[5,0,6],[3,7,2],[1,0,5],[3,6,0],[2,5,7],[6,7,1],[2,5,3],[1,4,7],[5,7,6],[7,6,4],[5,1,3],[7,4,6],[6,3,0],[3,1,7],[1,6,3],[4,2,7],[7,0,6],[6,4,1],[1,3,0],[7,2,6],[6,2,1],[4,5,3],[6,4,1],[5,6,2],[6,5,0],[2,0,3],[1,4,7],[7,1,4],[7,5,0],[3,4,1],[3,4,7],[1,2,4],[0,2,7],[3,4,0],[6,4,0],[7,5,3],[0,4,6],[5,4,0],[3,7,5],[4,6,3],[6,2,1],[3,4,0],[4,2,7],[4,3,5],[0,6,4],[3,1,0],[6,7,4],[1,6,4],[5,4,2],[6,5,1],[5,0,1],[3,5,7],[4,2,5],[6,5,1],[4,6,5],[1,3,5],[2,6,5],[1,0,6],[0,4,1],[3,4,7],[4,7,3],[6,4,0],[1,0,3],[3,4,1],[0,2,3],[3,2,6],[6,3,2],[5,7,2],[6,2,4],[0,5,1],[2,7,0],[3,2,4],[1,5,2],[5,4,2],[4,5,3],[2,7,0],[1,7,5],[5,1,0],[3,0,4],[4,1,5],[5,3,0],[1,7,3],[3,6,0],[1,6,5],[7,0,2],[6,3,5],[6,5,7],[5,7,3],[1,6,5],[3,4,2],[3,5,4],[1,0,7],[2,7,3],[6,0,5],[0,6,1],[3,5,1],[5,1,3],[5,4,0],[5,1,6],[3,6,4],[5,7,0],[2,5,4],[7,1,0],[6,4,5],[2,4,0],[4,2,1],[5,3,0],[7,6,2],[6,7,1],[1,3,6],[3,6,1],[1,2,7],[2,3,6],[3,1,4],[6,4,0],[2,5,3],[7,0,4],[4,3,7],[3,6,7],[3,6,4],[7,2,3],[4,7,6],[0,6,3],[3,1,5],[3,1,0],[1,3,0],[6,7,0],[2,6,4],[7,4,3],[4,7,3],[3,4,7],[3,0,2],[3,4,0],[7,1,5],[3,4,0],[1,3,4],[1,6,5],[2,1,0],[0,7,2],[6,1,5],[5,6,7],[0,2,6],[2,5,3],[5,2,6],[6,4,5],[2,5,0],[6,5,1],[4,7,0],[2,7,6],[1,2,4],[0,6,5],[7,0,6],[6,5,1],[7,6,1],[2,1,3],[7,2,4],[1,0,3],[5,1,0],[3,0,7],[6,3,5],[6,0,3],[0,4,1],[6,0,1],[5,0,7],[1,5,6],[4,2,5],[4,2,3],[4,5,0],[5,3,2],[4,3,7],[3,1,6],[6,2,1],[3,1,2],[3,4,5],[4,7,5],[3,0,7],[4,3,0],[3,0,4],[2,5,1],[6,5,1],[4,3,2],[6,5,2],[4,3,2],[2,3,1],[4,7,1],[7,2,1],[6,4,0],[6,4,1],[3,5,2],[4,7,6],[7,2,6],[3,5,7],[2,6,5],[7,6,5],[1,5,3],[2,7,1],[7,3,5],[2,4,3],[3,4,6],[1,5,3],[3,1,2],[3,5,0],[3,4,0],[3,7,0],[4,6,7],[6,7,1],[5,6,1],[0,3,6],[6,5,2],[3,7,6],[0,2,3],[5,4,1],[6,3,4],[2,7,6],[2,4,6],[3,6,5],[3,2,7],[6,1,3],[4,2,0],[7,1,5],[4,7,6],[4,6,5],[4,3,6],[4,6,5],[6,5,3],[0,6,3],[7,0,2],[4,3,6],[4,5,2],[3,0,6],[4,3,0],[3,4,6],[0,2,3],[4,3,6],[6,1,3],[1,0,6],[0,6,4],[0,4,3],[2,3,1],[5,3,0],[2,4,6],[2,3,0],[4,6,3],[4,6,0],[4,2,0],[4,6,1],[5,2,1],[6,4,0],[0,5,4],[5,7,6],[4,0,5],[6,7,5],[6,4,5],[2,3,6],[0,4,6],[2,3,7],[7,0,3],[0,5,6],[6,1,4],[0,2,5],[7,1,0],[2,7,0],[7,3,5],[3,6,0],[4,0,1],[7,0,4],[1,6,4],[0,2,1],[3,1,6],[2,7,5],[2,3,0],[6,7,3],[4,1,6],[2,4,0],[2,1,7],[2,7,0],[3,1,6],[6,4,5],[3,6,5],[2,3,4],[2,7,4],[1,4,0],[1,5,7],[6,0,4],[5,1,6],[3,6,7],[5,6,0],[5,1,2],[0,1,3],[5,7,3],[2,7,4],[1,6,2],[6,5,3],[6,4,2],[7,3,2],[2,4,3],[6,2,0],[6,0,1],[5,3,1],[3,6,2],[2,3,0],[0,1,5],[0,5,3],[6,3,2],[2,0,1],[1,0,6],[4,3,1],[4,2,7],[0,2,1],[4,6,7],[1,7,2],[7,4,2],[0,1,3],[6,4,1],[4,1,7],[6,7,2],[5,4,1],[2,6,4],[5,7,0],[3,0,4],[5,3,2],[6,1,7],[1,2,7],[6,2,5],[6,4,1],[0,6,3],[6,4,7],[1,5,6],[4,6,5],[7,6,4],[2,3,4],[7,1,2],[2,0,4],[1,3,6],[6,7,1],[1,6,3],[3,0,4],[5,2,7],[1,2,3],[3,5,0],[6,5,2],[3,0,6],[5,7,4],[7,0,6],[4,5,6],[2,5,0],[4,3,0],[2,7,0],[6,3,5],[6,7,4],[0,7,5],[3,7,6],[1,7,5],[6,4,3],[7,1,2],[1,4,3],[1,6,7],[7,5,6],[4,5,2],[1,3,0],[3,1,7],[2,3,6],[3,7,5],[1,3,4],[6,0,5],[4,7,2],[6,5,4],[2,6,1],[3,1,4],[3,2,0],[7,3,4],[3,0,2],[4,5,1],[3,7,6],[2,3,7],[4,5,7],[2,1,6],[1,3,0],[3,5,2],[4,7,3],[3,1,0],[6,0,2],[4,7,6],[1,0,3],[6,0,4],[1,4,0],[6,1,0],[7,2,4],[3,0,4],[2,6,4],[7,5,6],[4,1,3],[6,4,7],[5,6,7],[0,4,7],[6,5,3],[0,6,2],[5,7,3],[2,1,5],[0,7,3],[4,2,3],[4,1,0],[5,0,3],[5,7,3],[6,4,5],[3,5,6],[5,6,3],[3,6,7],[2,6,3],[2,3,6],[7,2,5],[3,5,7],[6,4,5],[4,1,7],[1,6,3],[1,3,0],[1,3,0],[6,0,3],[4,2,1],[4,2,1],[5,0,3],[3,6,7],[3,4,7],[2,5,3],[6,2,0],[4,2,6],[6,0,3],[7,1,6],[2,1,3],[4,5,0],[2,4,1],[5,1,0],[6,1,5],[0,7,5],[3,4,7],[4,1,5],[4,7,1],[4,7,2],[6,5,3],[2,3,5],[0,7,5],[7,3,1],[1,3,6],[7,5,6],[4,0,2],[2,1,6],[4,6,2],[5,3,0],[0,3,6],[3,6,5],[7,2,3],[1,2,4],[7,6,0],[4,5,1],[4,0,7],[5,2,4],[1,4,7],[0,7,2],[5,6,0],[4,6,3],[4,3,6],[1,2,5],[7,1,2],[1,7,4],[7,4,2],[5,0,4],[1,7,4],[7,2,0],[4,3,1],[6,2,5],[6,2,4],[1,4,7],[6,3,2],[7,6,5],[2,0,5],[7,3,1],[0,4,7],[3,1,4],[1,7,5],[3,1,2],[2,0,1],[5,0,2],[7,3,5],[6,4,0],[2,4,5],[4,6,0],[2,1,4],[0,4,5],[3,7,5],[7,6,2],[6,5,0],[6,7,3],[4,7,1],[3,2,6],[0,2,3],[0,1,2],[1,4,6],[6,7,4]]]
ZW = 1576
def setup_inputs(rng):
    return {"z": rng.standard_normal((N, 128, ZW), dtype=np.float32), "g": rng.random((N, 128, T * K), dtype=np.float32)}
def reference(z, g):
    y = np.zeros((N, 128, T), np.float64)
    fill = [0] * N
    for r in range(N):
        for t in range(T):
            for k, e in enumerate(ROUTE[r][t]):
                y[r][:, t] += g[r][:, t * K + k].astype(np.float64) * z[e][:, fill[e]].astype(np.float64)
                fill[e] += 1
    return {"y": y.astype(z.dtype)}

from concourse.mybir import AluOpType

SCRATCH = {
    "zs": ("sbuf", [128, 1576], "float32"),
    "gs": ("sbuf", [128, 1536], "float32"),
    "land": ("sbuf", [128, 1536], "float32"),
    "prod": ("sbuf", [128, 1536], "float32"),
    "part": ("sbuf", [128, 512], "float32"),
    "ys": ("sbuf", [128, 512], "float32"),
}
SEMAPHORES = ["zload", "gload", "arrived", "sent", "mul", "add1", "add2", "stored"]


def _plan(route, n, k_top):
    where = [[[] for _ in range(n)] for _ in range(n)]
    for r in range(n):
        for t, experts in enumerate(route[r]):
            for k, e in enumerate(experts):
                where[r][e].append(t * k_top + k)
    return where


def rank_program(g, core, T, topo):
    rank = T.rank_of(core)
    if rank is None:
        return
    cores = T.cores
    n = len(cores)
    k_top = T.tables["K"]
    where = _plan(T.tables["ROUTE"], n, k_top)
    cnt = [[len(where[r][e]) for r in range(n)] for e in range(n)]
    zoff = [[sum(cnt[e][:r]) for r in range(n)] for e in range(n)]
    loff = [[sum(cnt[x][r] for x in range(e)) for e in range(n)] for r in range(n)]
    used = sum(cnt[rank])
    sem = T.sem

    g.sync.dma_start(T.zs[:, 0:used], T.z[:, 0:used]).then_inc(sem.zload, 16)
    g.scalar.dma_start(T.gs[:], T.g[:]).then_inc(sem.gload, 16)

    g.wait_ge(sem.zload, 16)
    for step in range(1, n):
        r = (rank + step) % n
        rid, pid, _se = topo.addr(cores[r])
        g.remote_dma(
            T.land[:, loff[r][rank]:loff[r][rank] + cnt[rank][r]],
            T.zs[:, zoff[rank][r]:zoff[rank][r] + cnt[rank][r]],
            sem.arrived, sem.sent, pid, rid, topo.mask(core, cores[r]))

    v = g.vector
    v.wait_ge(sem.zload, 16)
    v.wait_ge(sem.gload, 16)
    v.wait_ge(sem.arrived, 16 * (n - 1))
    calls = 0
    for e in range(n):
        a = where[rank][e]
        buf, base = (T.zs, zoff[rank][rank]) if e == rank else (T.land, loff[rank][e])
        j = 0
        while j < len(a):
            i = j
            d = 1
            if j + 1 < len(a):
                d = a[j + 1] - a[j]
                i = j + 1
                while i + 1 < len(a) and a[i + 1] - a[i] == d:
                    i += 1
            v.tensor_tensor(T.prod[:, a[j]:a[i] + 1:d], buf[:, base + j:base + i + 1], T.gs[:, a[j]:a[i] + 1:d],
                            AluOpType.mult).then_inc(sem.mul, 1)
            calls += 1
            j = i + 1

    v.wait_ge(sem.mul, calls)
    v.tensor_tensor(T.part[:], T.prod[:, 0::k_top], T.prod[:, 1::k_top], AluOpType.add).then_inc(sem.add1, 1)
    v.wait_ge(sem.add1, 1)
    v.tensor_tensor(T.ys[:], T.part[:], T.prod[:, 2::k_top], AluOpType.add).then_inc(sem.add2, 1)

    g.sync.wait_ge(sem.add2, 1)
    g.sync.dma_start(T.y[:], T.ys[:]).then_inc(sem.stored, 16)
    g.sync.wait_ge(sem.stored, 16)

    g.wait_ge(sem.sent, 16 * (n - 1))
